import numpy as np, ml_dtypes
CORES = [26,28,98,100,106,108,122,124]
N = 8
import mx_ref
NC, KB = 128, 3
BF = ml_dtypes.bfloat16
def cut(t, i, w=512):
    return t[:, w * i:w * i + w]
def term(a, B):
    return np.stack([mx_ref.matmul(mx_ref.quantize(cut(a, i)), B) for i in range(4)], axis=2).reshape(128, -1)
def setup_inputs(rng):
    def f(*shape):
        return mx_ref.flush((rng.standard_normal(shape, dtype=np.float32) * np.exp2(rng.integers(-2, 3, shape[:-1] + (1,)))).astype(BF))
    return {"a": f(N, 128, 4 * 512), "b": f(N, 128, KB * 4 * NC)}
def setup_inputs_blocks(rng):
    d = setup_inputs(rng)
    for k in ("a", "b"): d[k] = mx_ref.spread(d[k], rng, 2)
    return d
def setup_inputs_wide(rng):
    d = setup_inputs(rng)
    for k in ("a", "b"): d[k] = mx_ref.flush((d[k].astype(np.float32) * np.exp2(rng.integers(-4, 5, (N, 1, 1))).astype(np.float32)).astype(BF))
    return d
def setup_inputs_lossless(rng):
    a = np.zeros((N, 128, 4 * 128, 4), np.float32)
    for r in range(N):
        k = rng.integers(0, 512, size=4 * 128)
        a[r, k // 4, np.arange(4 * 128), k % 4] = 1.0
    size = np.repeat(2.0 ** rng.integers(-4, 5, size=(1, 1, (KB * 4 * NC) // 4)), 4, axis=2)
    b = rng.integers(-1, 2, size=(N, 128, KB * 4 * NC)) * size
    return {"a": a.reshape(N, 128, 4 * 512).astype(BF), "b": b.astype(np.float32).astype(BF)}
def reference(a, b):
    y = np.zeros((N, 128, KB * 4 * NC), np.float32)
    for k in range(KB):
        y[:, :, 4 * NC * k:4 * NC * k + 4 * NC] = mx_ref.total([term(a[r], mx_ref.quantize(cut(b[r], k, 4 * NC))) for r in range(N)])
    return {"y": y}

@@ -1,0 +1,262 @@
+from concourse.bass import DstId, RemoteDMATransfer
+from concourse.mybir import dt, AluOpType, ActivationFunctionType
+
+W = 384
+PIECES = [(0, 192), (192, 384)]
+NX = 72
+
+
+def _pair(name, n):
+    return {name + "c": ("sbuf", [128, n], "float8_e4m3fn_x4"), name + "p": ("sbuf", [128, n], "uint8")}
+
+
+SCRATCH = {
+    "at": ("sbuf", [128, 2048], "bfloat16"),
+    "bt": ("sbuf", [128, 1536], "bfloat16"),
+    "ones": ("sbuf", [128, 512], "bfloat16"),
+    "selt": ("sbuf", [128, 2048], "bfloat16"),
+    "tt": ("sbuf", [128, 1536], "bfloat16"),
+    "ut": ("sbuf", [128, 1536], "bfloat16"),
+    "vt": ("sbuf", [128, 1536], "bfloat16"),
+    "yt": ("sbuf", [128, 1536], "float32"),
+    "ps": ("psum", [128, 4096], "float32"),
+}
+for _n, _w in (("a", 512), ("b", W), ("sel", 512), ("t", W), ("u", W), ("v", W), ("l0", W), ("l1", W),
+               ("r0", W), ("r1", W), ("r2", W), ("r3", W), ("f", W)):
+    SCRATCH.update(_pair(_n, _w))
+
+SEMAPHORES = (["x%d" % i for i in range(NX)] + ["sl%d_%d" % (k, j) for k in range(2) for j in range(2)]
+              + ["sr%d_%d" % (c, j) for c in range(4) for j in range(2)] + ["sf0", "sf1", "loc"])
+
+
+def _bits(mask):
+    return bin(mask).count("1")
+
+
+def _pick(mask, k, skip=0):
+    on = [i for i in range(mask.bit_length()) if (mask >> i) & 1]
+    return sum(1 << i for i in on[skip:skip + k])
+
+
+def _common(topo, src, dests):
+    m = topo.mask(src, dests[0])
+    for d in dests[1:]:
+        m &= topo.mask(src, d)
+    return m
+
+
+def _pow2(n):
+    p = 1
+    while 2 * p <= n:
+        p *= 2
+    return p
+
+
+def _plan(T, topo):
+    cores = list(T.cores)
+    chips = []
+    for c in cores:
+        if topo.chip(c) not in chips:
+            chips.append(topo.chip(c))
+    ranks = {x: [c for c in cores if topo.chip(c) == x] for x in chips}
+
+    def free(c):
+        return all(topo.may_write(c, d) for d in cores if d != c)
+
+    agent = {}
+    for x in chips:
+        agent[x] = []
+        for own in ranks[x]:
+            if free(own):
+                agent[x].append(own)
+            else:
+                agent[x].append([c for c in range(topo.CHIPS * topo.CORES_PER_CHIP)
+                                 if topo.chip(c) == x and topo.die(c) == topo.die(own) and c not in cores and free(c)][0])
+    return chips, ranks, agent
+
+
+def rank_program(g, core, T, topo):
+    chips, ranks, agent = _plan(T, topo)
+    x = topo.chip(core)
+    if x not in chips:
+        return
+    is_rank = T.rank_of(core) is not None
+    if not is_rank and core not in agent[x]:
+        return
+    Q = {"t": g.tensor, "v": g.vector, "s": g.scalar, "y": g.sync, "g": g}
+    st = {"n": 0, "set": 0, "free": [[], []], "loc": 0, "seen": {}}
+
+    def new():
+        st["n"] += 1
+        return "x%d" % (st["n"] - 1)
+
+    def wait(q, name, val):
+        if st["seen"].get((q, name), 0) < val:
+            st["seen"][(q, name)] = val
+            Q[q].wait_ge(T.sem[name], val)
+
+    def step1(xx, k):
+        r = ranks[xx][k]
+        out = []
+        for j in range(2):
+            d = []
+            for c in (agent[xx][j], ranks[xx][j]):
+                if c != r and c not in d:
+                    d.append(c)
+            if d:
+                out.append((j, d))
+        m = _common(topo, r, [c for (_, d) in out for c in d])
+        per = _pow2(_bits(m) // len(out))
+        return [(j, d, _pick(m, per, per * i)) for i, (j, d) in enumerate(out)]
+
+    def count1(xx, k, j):
+        return [2 * _bits(m) for (jj, _, m) in step1(xx, k) if jj == j][0]
+
+    def step2(xx, j):
+        d = [ranks[yy][j] for yy in chips if yy != xx]
+        m = _common(topo, agent[xx][j], d)
+        return d, _pick(m, _pow2(_bits(m)))
+
+    def step3(xx, j):
+        d = [c for c in ranks[xx] if c != ranks[xx][j]]
+        m = _common(topo, ranks[xx][j], d)
+        return d, _pick(m, _pow2(_bits(m)))
+
+    if is_rank:
+        ld_b, ld_a = new(), [new() for _ in range(4)]
+        g.sync.dma_start(T.bt[:, :], T.b[:, :]).then_inc(T.sem[ld_b], 16)
+        for i in range(4):
+            q = g.scalar if i % 2 == 0 else g.sync
+            q.dma_start(T.at[:, 512 * i:512 * i + 512], T.a[:, 512 * i:512 * i + 512]).then_inc(T.sem[ld_a[i]], 16)
+
+    s_one, s_zero, s_aff, s_sh, s_sel = new(), new(), new(), new(), new()
+    g.vector.memset(T.ones[:, :], 1.0).then_inc(T.sem[s_one], 1)
+    g.vector.memset(T.selt[:, 512:2048], 0.0).then_inc(T.sem[s_zero], 1)
+    wait("g", s_one, 1)
+    g.affine_select(T.selt[:, 0:512], T.ones[:, :], [[-1, 512]], AluOpType.is_equal, 0.0, 0, 4).then_inc(T.sem[s_aff], 1)
+    wait("v", s_zero, 1)
+    wait("v", s_aff, 1)
+    for t in range(1, 4):
+        g.vector.tensor_copy(T.selt[:, 512 * t + t:512 * t + 512], T.selt[:, 0:512 - t]).then_inc(T.sem[s_sh], 1)
+    wait("v", s_sh, 3)
+    g.vector.quantize_mx(T.selc[:, :], T.selp[:, :], T.selt[:, :]).then_inc(T.sem[s_sel], 1)
+
+    if is_rank:
+        q_b, q_a = new(), [new() for _ in range(4)]
+        wait("v", ld_b, 16)
+        g.vector.quantize_mx(T.bc[:, :], T.bp[:, :], T.bt[:, :]).then_inc(T.sem[q_b], 1)
+        for i in range(4):
+            wait("v", ld_a[i], 16)
+            g.vector.quantize_mx(T.ac[:, 128 * i:128 * i + 128], T.ap[:, 128 * i:128 * i + 128],
+                                 T.at[:, 512 * i:512 * i + 512]).then_inc(T.sem[q_a[i]], 1)
+
+    def add_up(w0, w1, parts):
+        s = st["set"]
+        st["set"] = 1 - s
+        for (name, val) in st["free"][s]:
+            wait("t", name, val)
+        st["free"][s] = []
+        done = [new() for _ in range(4)]
+        for k, part in enumerate(parts):
+            for t in range(4):
+                if part is None:
+                    wait("t", q_b, 1)
+                    wait("t", q_a[t], 1)
+                    lc, lp, rc, rp = T.ac, T.ap, T.bc, T.bp
+                else:
+                    wait("t", s_sel, 1)
+                    wait("t", part[1], part[2])
+                    lc, lp, rc, rp = T.selc, T.selp, T[part[0] + "c"], T[part[0] + "p"]
+                c0 = 512 * (4 * s + t)
+                ins = g.tensor.matmul_mx(T.ps[:, c0:c0 + w1 - w0], lc[:, 128 * t:128 * t + 128],
+                                         lp[:, 128 * t:128 * t + 128], rc[:, w0:w1], rp[:, w0:w1],
+                                         k == 0, k == len(parts) - 1)
+                if k == len(parts) - 1:
+                    ins.then_inc(T.sem[done[t]], 1)
+        return s, done
+
+    def take_out(job, w0, w1, tile):
+        s, done = job
+        cp = new()
+        for t in range(4):
+            c0 = 512 * (4 * s + t)
+            src, dst = T.ps[:, c0:c0 + w1 - w0], tile[:, 4 * w0 + t:4 * w1:4]
+            if t % 2 == 0:
+                wait("s", done[t], 1)
+                g.scalar.activation(dst, src, ActivationFunctionType.Copy).then_inc(T.sem[cp], 1)
+            else:
+                wait("v", done[t], 1)
+                g.vector.tensor_copy(dst, src).then_inc(T.sem[cp], 1)
+        st["free"][s].append((cp, 4))
+        return cp
+
+    def pack(cp, name, w0, w1):
+        q = new()
+        wait("v", cp, 4)
+        g.vector.quantize_mx(T[name + "c"][:, w0:w1], T[name + "p"][:, w0:w1],
+                             T[name + "t"][:, 4 * w0:4 * w1]).then_inc(T.sem[q], 1)
+        return q
+
+    def send(q, name, trs):
+        wait("g", q, 1)
+        for kind in ("c", "p"):
+            lst = []
+            for (j, dests, mask, land, sem) in trs:
+                w0, w1 = PIECES[j]
+                src, dst = T[name + kind][:, w0:w1], T[land + kind][:, w0:w1]
+                if kind == "c":
+                    src, dst = src.bitcast(dt.uint8), dst.bitcast(dt.uint8)
+                lst.append(RemoteDMATransfer(dst_ids=[DstId(rid=topo.addr(d)[0], pnc=topo.addr(d)[1]) for d in dests],
+                                             dma_engine_mask=mask, remote_sem=T.sem[sem], srcs=[src],
+                                             dsts=[dst for _ in dests]))
+                st["loc"] += _bits(mask)
+            g.remote_dma_fused(lst, local_sem=T.sem.loc)
+
+    def landed1(k, j):
+        return ("l%d" % k, "sl%d_%d" % (k, j), count1(x, k, j))
+
+    def chip_sum(j, parts):
+        w0, w1 = PIECES[j]
+        q = pack(take_out(add_up(w0, w1, parts), w0, w1, T.ut), "u", w0, w1)
+        d, m = step2(x, j)
+        send(q, "u", [(j, d, m, "r%d" % chips.index(x), "sr%d_%d" % (chips.index(x), j))])
+
+    stores = []
+
+    def store(cp, w0, w1):
+        s = new()
+        wait("y", cp, 4)
+        g.sync.dma_start(T.y[:, 4 * w0:4 * w1], T.yt[:, 4 * w0:4 * w1]).then_inc(T.sem[s], 16)
+        stores.append(s)
+
+    if not is_rank:
+        for j in range(2):
+            if agent[x][j] == core:
+                chip_sum(j, [landed1(0, j), landed1(1, j)])
+    else:
+        k = ranks[x].index(core)
+        mine, other = k, 1 - k
+        trs = step1(x, k)
+        w0, w1 = min(PIECES[j][0] for (j, _, _) in trs), max(PIECES[j][1] for (j, _, _) in trs)
+        q = pack(take_out(add_up(w0, w1, [None]), w0, w1, T.tt), "t", w0, w1)
+        send(q, "t", [(j, d, m, "l%d" % k, "sl%d_%d" % (k, j)) for (j, d, m) in trs])
+        if agent[x][mine] == core:
+            chip_sum(mine, [None, landed1(other, mine)])
+        w0, w1 = PIECES[mine]
+        far = sorted([yy for yy in chips if yy != x],
+                     key=lambda yy: 0 if (topo.mates(yy, x) or topo.same_plane(yy, x)) else 1)
+        parts = [None, landed1(other, mine)]
+        for yy in far:
+            parts.append(("r%d" % chips.index(yy), "sr%d_%d" % (chips.index(yy), mine), 2 * _bits(step2(yy, mine)[1])))
+        job = add_up(w0, w1, parts)
+        q = pack(take_out(job, w0, w1, T.vt), "v", w0, w1)
+        d, m = step3(x, mine)
+        send(q, "v", [(mine, d, m, "f", "sf%d" % mine)])
+        store(take_out(job, w0, w1, T.yt), w0, w1)
+        w0, w1 = PIECES[other]
+        job = add_up(w0, w1, [("f", "sf%d" % other, 2 * _bits(step3(x, other)[1]))])
+        store(take_out(job, w0, w1, T.yt), w0, w1)
+
+    wait("g", "loc", st["loc"])
+    for s in stores:
+        wait("y", s, 16)

@@ -2,8 +2,9 @@ from concourse.bass import DstId, RemoteDMATransfer
 from concourse.mybir import dt, AluOpType, ActivationFunctionType
 
 W = 384
-PIECES = [(0, 192), (192, 384)]
-NX = 72
+PIECES = [(0, 128), (128, 256), (256, 384)]
+NP = 3
+NX = 90
 
 
 def _pair(name, n):
@@ -25,8 +26,8 @@ for _n, _w in (("a", 512), ("b", W), ("sel", 512), ("t", W), ("u", W), ("v", W),
                ("r0", W), ("r1", W), ("r2", W), ("r3", W), ("f", W)):
     SCRATCH.update(_pair(_n, _w))
 
-SEMAPHORES = (["x%d" % i for i in range(NX)] + ["sl%d_%d" % (k, j) for k in range(2) for j in range(2)]
-              + ["sr%d_%d" % (c, j) for c in range(4) for j in range(2)] + ["sf0", "sf1", "loc"])
+SEMAPHORES = (["x%d" % i for i in range(NX)] + ["sl%d_%d" % (k, j) for k in range(2) for j in range(NP)]
+              + ["sr%d_%d" % (c, j) for c in range(4) for j in range(NP)] + ["sf%d" % j for j in range(NP)] + ["loc"])
 
 
 def _bits(mask):
@@ -63,25 +64,32 @@ def _plan(T, topo):
     def free(c):
         return all(topo.may_write(c, d) for d in cores if d != c)
 
-    agent = {}
+    owner, agent = {}, {}
     for x in chips:
-        agent[x] = []
-        for own in ranks[x]:
-            if free(own):
-                agent[x].append(own)
-            else:
-                agent[x].append([c for c in range(topo.CHIPS * topo.CORES_PER_CHIP)
-                                 if topo.chip(c) == x and topo.die(c) == topo.die(own) and c not in cores and free(c)][0])
-    return chips, ranks, agent
+        used = []
+
+        def helper(die):
+            h = [c for c in range(topo.CHIPS * topo.CORES_PER_CHIP) if topo.chip(c) == x and topo.die(c) == die
+                 and c not in cores and c not in used and free(c)][0]
+            used.append(h)
+            return h
+
+        owner[x] = list(ranks[x])
+        agent[x] = [r if free(r) else helper(topo.die(r)) for r in ranks[x]]
+        early = [r for r in ranks[x] if free(r)] + list(ranks[x])
+        h = helper(topo.die(early[0]))
+        owner[x].append(h)
+        agent[x].append(h)
+    return chips, ranks, owner, agent
 
 
 def rank_program(g, core, T, topo):
-    chips, ranks, agent = _plan(T, topo)
+    chips, ranks, owner, agent = _plan(T, topo)
     x = topo.chip(core)
     if x not in chips:
         return
     is_rank = T.rank_of(core) is not None
-    if not is_rank and core not in agent[x]:
+    if not is_rank and core not in agent[x] and core not in owner[x]:
         return
     Q = {"t": g.tensor, "v": g.vector, "s": g.scalar, "y": g.sync, "g": g}
     st = {"n": 0, "set": 0, "free": [[], []], "loc": 0, "seen": {}}
@@ -95,58 +103,89 @@ def rank_program(g, core, T, topo):
             st["seen"][(q, name)] = val
             Q[q].wait_ge(T.sem[name], val)
 
+    def outside(xx, j):
+        return agent[xx][j] not in ranks[xx]
+
     def step1(xx, k):
         r = ranks[xx][k]
+        groups = {"early": [], "again": [], "late": []}
+        for j in range(NP):
+            a, o = agent[xx][j], owner[xx][j]
+            if outside(xx, j):
+                groups["early"].append((j, [a]))
+                if o != a and o != r:
+                    groups["again"].append((j, [o]))
+            else:
+                d = []
+                for c in (a, o):
+                    if c != r and c not in d:
+                        d.append(c)
+                if d:
+                    groups["late"].append((j, d))
         out = []
-        for j in range(2):
-            d = []
-            for c in (agent[xx][j], ranks[xx][j]):
-                if c != r and c not in d:
-                    d.append(c)
-            if d:
-                out.append((j, d))
-        m = _common(topo, r, [c for (_, d) in out for c in d])
-        per = _pow2(_bits(m) // len(out))
-        return [(j, d, _pick(m, per, per * i)) for i, (j, d) in enumerate(out)]
+        for kind in ("early", "again", "late"):
+            grp = groups[kind]
+            if grp:
+                m = _common(topo, r, [c for (_, d) in grp for c in d])
+                per = _pow2(_bits(m) // len(grp))
+                out.append((kind, [(j, d, _pick(m, per, per * i)) for i, (j, d) in enumerate(grp)]))
+        return out
 
     def count1(xx, k, j):
-        return [2 * _bits(m) for (jj, _, m) in step1(xx, k) if jj == j][0]
+        return [2 * _bits(m) for (_, grp) in step1(xx, k) for (jj, d, m) in grp if jj == j and core in d][0]
 
     def step2(xx, j):
-        d = [ranks[yy][j] for yy in chips if yy != xx]
+        d = [owner[yy][j] for yy in chips if yy != xx]
         m = _common(topo, agent[xx][j], d)
         return d, _pick(m, _pow2(_bits(m)))
 
     def step3(xx, j):
-        d = [c for c in ranks[xx] if c != ranks[xx][j]]
-        m = _common(topo, ranks[xx][j], d)
+        d = [c for c in ranks[xx] if c != owner[xx][j]]
+        m = _common(topo, owner[xx][j], d)
         return d, _pick(m, _pow2(_bits(m)))
 
     if is_rank:
-        ld_b, ld_a = new(), [new() for _ in range(4)]
-        g.sync.dma_start(T.bt[:, :], T.b[:, :]).then_inc(T.sem[ld_b], 16)
-        for i in range(4):
-            q = g.scalar if i % 2 == 0 else g.sync
-            q.dma_start(T.at[:, 512 * i:512 * i + 512], T.a[:, 512 * i:512 * i + 512]).then_inc(T.sem[ld_a[i]], 16)
+        first = [j for j in range(NP) if outside(x, j)]
+        b_parts = [(min(PIECES[j][0] for j in first), max(PIECES[j][1] for j in first))]
+        b_parts += [PIECES[j] for j in range(NP) if j not in first]
+        loads = [(T.bt, T.b, 4 * b_parts[0][0], 4 * b_parts[0][1])]
+        loads += [(T.at, T.a, 512 * i, 512 * i + 512) for i in range(4)]
+        loads += [(T.bt, T.b, 4 * w0, 4 * w1) for (w0, w1) in b_parts[1:]]
+        ld = []
+        for i, (dst, src, c0, c1) in enumerate(loads):
+            ld.append(new())
+            (g.sync if i % 2 == 0 or i > 4 else g.scalar).dma_start(dst[:, c0:c1], src[:, c0:c1]).then_inc(T.sem[ld[i]], 16)
 
     s_one, s_zero, s_aff, s_sh, s_sel = new(), new(), new(), new(), new()
     g.vector.memset(T.ones[:, :], 1.0).then_inc(T.sem[s_one], 1)
     g.vector.memset(T.selt[:, 512:2048], 0.0).then_inc(T.sem[s_zero], 1)
     wait("g", s_one, 1)
     g.affine_select(T.selt[:, 0:512], T.ones[:, :], [[-1, 512]], AluOpType.is_equal, 0.0, 0, 4).then_inc(T.sem[s_aff], 1)
-    wait("v", s_zero, 1)
-    wait("v", s_aff, 1)
-    for t in range(1, 4):
-        g.vector.tensor_copy(T.selt[:, 512 * t + t:512 * t + 512], T.selt[:, 0:512 - t]).then_inc(T.sem[s_sh], 1)
-    wait("v", s_sh, 3)
-    g.vector.quantize_mx(T.selc[:, :], T.selp[:, :], T.selt[:, :]).then_inc(T.sem[s_sel], 1)
+
+    def finish_picks():
+        wait("v", s_zero, 1)
+        wait("v", s_aff, 1)
+        for t in range(1, 4):
+            g.vector.tensor_copy(T.selt[:, 512 * t + t:512 * t + 512], T.selt[:, 0:512 - t]).then_inc(T.sem[s_sh], 1)
+        wait("v", s_sh, 3)
+        g.vector.quantize_mx(T.selc[:, :], T.selp[:, :], T.selt[:, :]).then_inc(T.sem[s_sel], 1)
+
+    if not is_rank:
+        finish_picks()
+
+    q_b, q_a = [], []
+
+    def pack_b(i, sem):
+        w0, w1 = b_parts[i]
+        q_b.append((w0, w1, new()))
+        wait("v", sem, 16)
+        g.vector.quantize_mx(T.bc[:, w0:w1], T.bp[:, w0:w1], T.bt[:, 4 * w0:4 * w1]).then_inc(T.sem[q_b[-1][2]], 1)
 
     if is_rank:
-        q_b, q_a = new(), [new() for _ in range(4)]
-        wait("v", ld_b, 16)
-        g.vector.quantize_mx(T.bc[:, :], T.bp[:, :], T.bt[:, :]).then_inc(T.sem[q_b], 1)
+        pack_b(0, ld[0])
         for i in range(4):
-            wait("v", ld_a[i], 16)
+            q_a.append(new())
+            wait("v", ld[1 + i], 16)
             g.vector.quantize_mx(T.ac[:, 128 * i:128 * i + 128], T.ap[:, 128 * i:128 * i + 128],
                                  T.at[:, 512 * i:512 * i + 512]).then_inc(T.sem[q_a[i]], 1)
 
@@ -160,7 +199,9 @@ def rank_program(g, core, T, topo):
         for k, part in enumerate(parts):
             for t in range(4):
                 if part is None:
-                    wait("t", q_b, 1)
+                    for (v0, v1, sem) in q_b:
+                        if v0 < w1 and w0 < v1:
+                            wait("t", sem, 1)
                     wait("t", q_a[t], 1)
                     lc, lp, rc, rp = T.ac, T.ap, T.bc, T.bp
                 else:
@@ -212,14 +253,8 @@ def rank_program(g, core, T, topo):
                 st["loc"] += _bits(mask)
             g.remote_dma_fused(lst, local_sem=T.sem.loc)
 
-    def landed1(k, j):
-        return ("l%d" % k, "sl%d_%d" % (k, j), count1(x, k, j))
-
-    def chip_sum(j, parts):
-        w0, w1 = PIECES[j]
-        q = pack(take_out(add_up(w0, w1, parts), w0, w1, T.ut), "u", w0, w1)
-        d, m = step2(x, j)
-        send(q, "u", [(j, d, m, "r%d" % chips.index(x), "sr%d_%d" % (chips.index(x), j))])
+    def chip_parts(j):
+        return [None if r == core else ("l%d" % k, "sl%d_%d" % (k, j), count1(x, k, j)) for k, r in enumerate(ranks[x])]
 
     stores = []
 
@@ -229,33 +264,51 @@ def rank_program(g, core, T, topo):
         g.sync.dma_start(T.y[:, 4 * w0:4 * w1], T.yt[:, 4 * w0:4 * w1]).then_inc(T.sem[s], 16)
         stores.append(s)
 
-    if not is_rank:
-        for j in range(2):
-            if agent[x][j] == core:
-                chip_sum(j, [landed1(0, j), landed1(1, j)])
-    else:
+    if is_rank:
         k = ranks[x].index(core)
-        mine, other = k, 1 - k
-        trs = step1(x, k)
-        w0, w1 = min(PIECES[j][0] for (j, _, _) in trs), max(PIECES[j][1] for (j, _, _) in trs)
-        q = pack(take_out(add_up(w0, w1, [None]), w0, w1, T.tt), "t", w0, w1)
-        send(q, "t", [(j, d, m, "l%d" % k, "sl%d_%d" % (k, j)) for (j, d, m) in trs])
-        if agent[x][mine] == core:
-            chip_sum(mine, [None, landed1(other, mine)])
-        w0, w1 = PIECES[mine]
-        far = sorted([yy for yy in chips if yy != x],
-                     key=lambda yy: 0 if (topo.mates(yy, x) or topo.same_plane(yy, x)) else 1)
-        parts = [None, landed1(other, mine)]
-        for yy in far:
-            parts.append(("r%d" % chips.index(yy), "sr%d_%d" % (chips.index(yy), mine), 2 * _bits(step2(yy, mine)[1])))
-        job = add_up(w0, w1, parts)
-        q = pack(take_out(job, w0, w1, T.vt), "v", w0, w1)
-        d, m = step3(x, mine)
-        send(q, "v", [(mine, d, m, "f", "sf%d" % mine)])
-        store(take_out(job, w0, w1, T.yt), w0, w1)
-        w0, w1 = PIECES[other]
-        job = add_up(w0, w1, [("f", "sf%d" % other, 2 * _bits(step3(x, other)[1]))])
-        store(take_out(job, w0, w1, T.yt), w0, w1)
+        packed = {}
+        for kind, grp in step1(x, k):
+            if kind == "late":
+                for n in range(1, len(b_parts)):
+                    pack_b(n, ld[4 + n])
+            if kind != "again":
+                w0, w1 = min(PIECES[j][0] for (j, _, _) in grp), max(PIECES[j][1] for (j, _, _) in grp)
+                q = pack(take_out(add_up(w0, w1, [None]), w0, w1, T.tt), "t", w0, w1)
+                for (j, _, _) in grp:
+                    packed[j] = q
+            send(packed[grp[0][0]], "t", [(j, d, m, "l%d" % k, "sl%d_%d" % (k, j)) for (j, d, m) in grp])
+        for n in range(len(q_b), len(b_parts)):
+            pack_b(n, ld[4 + n])
+        finish_picks()
+
+    ci = chips.index(x)
+    for j in range(NP):
+        if agent[x][j] == core:
+            w0, w1 = PIECES[j]
+            q = pack(take_out(add_up(w0, w1, chip_parts(j)), w0, w1, T.ut), "u", w0, w1)
+            d, m = step2(x, j)
+            send(q, "u", [(j, d, m, "r%d" % ci, "sr%d_%d" % (ci, j))])
+
+    far = sorted([yy for yy in chips if yy != x],
+                 key=lambda yy: 0 if (topo.mates(yy, x) or topo.same_plane(yy, x)) else 1)
+    for j in range(NP):
+        if owner[x][j] == core:
+            w0, w1 = PIECES[j]
+            parts = chip_parts(j)
+            for yy in far:
+                parts.append(("r%d" % chips.index(yy), "sr%d_%d" % (chips.index(yy), j), 2 * _bits(step2(yy, j)[1])))
+            job = add_up(w0, w1, parts)
+            q = pack(take_out(job, w0, w1, T.vt), "v", w0, w1)
+            d, m = step3(x, j)
+            send(q, "v", [(j, d, m, "f", "sf%d" % j)])
+            if is_rank:
+                store(take_out(job, w0, w1, T.yt), w0, w1)
+
+    if is_rank:
+        for j in sorted([j for j in range(NP) if owner[x][j] != core], key=lambda j: 1 if outside(x, j) else 0):
+            w0, w1 = PIECES[j]
+            job = add_up(w0, w1, [("f", "sf%d" % j, 2 * _bits(step3(x, j)[1]))])
+            store(take_out(job, w0, w1, T.yt), w0, w1)
 
     wait("g", "loc", st["loc"])
     for s in stores:

@@ -27,7 +27,7 @@ for _n, _w in (("a", 512), ("b", W), ("sel", 512), ("t", W), ("u", W), ("v", W),
     SCRATCH.update(_pair(_n, _w))
 
 SEMAPHORES = (["x%d" % i for i in range(NX)] + ["sl%d_%d" % (k, j) for k in range(2) for j in range(NP)]
-              + ["sr%d_%d" % (c, j) for c in range(4) for j in range(NP)] + ["sf%d" % j for j in range(NP)] + ["loc"])
+              + ["sr%d_%d" % (c, j) for c in range(4) for j in range(NP)] + ["sf%d" % j for j in range(NP)] + ["sp", "loc"])
 
 
 def _bits(mask):
@@ -64,7 +64,7 @@ def _plan(T, topo):
     def free(c):
         return all(topo.may_write(c, d) for d in cores if d != c)
 
-    owner, agent = {}, {}
+    owner, agent, pal = {}, {}, {}
     for x in chips:
         used = []
 
@@ -80,11 +80,15 @@ def _plan(T, topo):
         h = helper(topo.die(early[0]))
         owner[x].append(h)
         agent[x].append(h)
-    return chips, ranks, owner, agent
+        for r in ranks[x]:
+            left = [c for c in used if c not in pal]
+            p = ([c for c in left if topo.die(c) == topo.die(r)] + left)[0]
+            pal[r], pal[p] = p, r
+    return chips, ranks, owner, agent, pal
 
 
 def rank_program(g, core, T, topo):
-    chips, ranks, owner, agent = _plan(T, topo)
+    chips, ranks, owner, agent, pal = _plan(T, topo)
     x = topo.chip(core)
     if x not in chips:
         return
@@ -156,22 +160,41 @@ def rank_program(g, core, T, topo):
             ld.append(new())
             (g.sync if i % 2 == 0 or i > 4 else g.scalar).dma_start(dst[:, c0:c1], src[:, c0:c1]).then_inc(T.sem[ld[i]], 16)
 
+    def send(q, name, trs):
+        wait("g", q, 1)
+        for kind in ("c", "p"):
+            lst = []
+            for ((w0, w1), dests, mask, land, sem) in trs:
+                src, dst = T[name + kind][:, w0:w1], T[land + kind][:, w0:w1]
+                if kind == "c":
+                    src, dst = src.bitcast(dt.uint8), dst.bitcast(dt.uint8)
+                lst.append(RemoteDMATransfer(dst_ids=[DstId(rid=topo.addr(d)[0], pnc=topo.addr(d)[1]) for d in dests],
+                                             dma_engine_mask=mask, remote_sem=T.sem[sem], srcs=[src],
+                                             dsts=[dst for _ in dests]))
+                st["loc"] += _bits(mask)
+            g.remote_dma_fused(lst, local_sem=T.sem.loc)
+
     s_one, s_zero, s_aff, s_sh, s_sel = new(), new(), new(), new(), new()
     g.vector.memset(T.ones[:, :], 1.0).then_inc(T.sem[s_one], 1)
-    g.vector.memset(T.selt[:, 512:2048], 0.0).then_inc(T.sem[s_zero], 1)
+    if not is_rank:
+        g.vector.memset(T.selt[:, 512:2048], 0.0).then_inc(T.sem[s_zero], 1)
     wait("g", s_one, 1)
     g.affine_select(T.selt[:, 0:512], T.ones[:, :], [[-1, 512]], AluOpType.is_equal, 0.0, 0, 4).then_inc(T.sem[s_aff], 1)
-
-    def finish_picks():
+    wait("v", s_aff, 1)
+    made = (0, 128) if is_rank else (128, 512)
+    if not is_rank:
         wait("v", s_zero, 1)
-        wait("v", s_aff, 1)
         for t in range(1, 4):
             g.vector.tensor_copy(T.selt[:, 512 * t + t:512 * t + 512], T.selt[:, 0:512 - t]).then_inc(T.sem[s_sh], 1)
         wait("v", s_sh, 3)
-        g.vector.quantize_mx(T.selc[:, :], T.selp[:, :], T.selt[:, :]).then_inc(T.sem[s_sel], 1)
+    g.vector.quantize_mx(T.selc[:, made[0]:made[1]], T.selp[:, made[0]:made[1]],
+                         T.selt[:, 4 * made[0]:4 * made[1]]).then_inc(T.sem[s_sel], 1)
 
-    if not is_rank:
-        finish_picks()
+    def swap_mask(src):
+        m = topo.mask(src, pal[src])
+        return _pick(m, _pow2(_bits(m)))
+
+    send(s_sel, "sel", [(made, [pal[core]], swap_mask(core), "sel", "sp")])
 
     q_b, q_a = [], []
 
@@ -206,6 +229,7 @@ def rank_program(g, core, T, topo):
                     lc, lp, rc, rp = T.ac, T.ap, T.bc, T.bp
                 else:
                     wait("t", s_sel, 1)
+                    wait("t", "sp", 2 * _bits(swap_mask(pal[core])))
                     wait("t", part[1], part[2])
                     lc, lp, rc, rp = T.selc, T.selp, T[part[0] + "c"], T[part[0] + "p"]
                 c0 = 512 * (4 * s + t)
@@ -238,21 +262,6 @@ def rank_program(g, core, T, topo):
                              T[name + "t"][:, 4 * w0:4 * w1]).then_inc(T.sem[q], 1)
         return q
 
-    def send(q, name, trs):
-        wait("g", q, 1)
-        for kind in ("c", "p"):
-            lst = []
-            for (j, dests, mask, land, sem) in trs:
-                w0, w1 = PIECES[j]
-                src, dst = T[name + kind][:, w0:w1], T[land + kind][:, w0:w1]
-                if kind == "c":
-                    src, dst = src.bitcast(dt.uint8), dst.bitcast(dt.uint8)
-                lst.append(RemoteDMATransfer(dst_ids=[DstId(rid=topo.addr(d)[0], pnc=topo.addr(d)[1]) for d in dests],
-                                             dma_engine_mask=mask, remote_sem=T.sem[sem], srcs=[src],
-                                             dsts=[dst for _ in dests]))
-                st["loc"] += _bits(mask)
-            g.remote_dma_fused(lst, local_sem=T.sem.loc)
-
     def chip_parts(j):
         return [None if r == core else ("l%d" % k, "sl%d_%d" % (k, j), count1(x, k, j)) for k, r in enumerate(ranks[x])]
 
@@ -276,10 +285,9 @@ def rank_program(g, core, T, topo):
                 q = pack(take_out(add_up(w0, w1, [None]), w0, w1, T.tt), "t", w0, w1)
                 for (j, _, _) in grp:
                     packed[j] = q
-            send(packed[grp[0][0]], "t", [(j, d, m, "l%d" % k, "sl%d_%d" % (k, j)) for (j, d, m) in grp])
+            send(packed[grp[0][0]], "t", [(PIECES[j], d, m, "l%d" % k, "sl%d_%d" % (k, j)) for (j, d, m) in grp])
         for n in range(len(q_b), len(b_parts)):
             pack_b(n, ld[4 + n])
-        finish_picks()
 
     ci = chips.index(x)
     for j in range(NP):
@@ -287,7 +295,7 @@ def rank_program(g, core, T, topo):
             w0, w1 = PIECES[j]
             q = pack(take_out(add_up(w0, w1, chip_parts(j)), w0, w1, T.ut), "u", w0, w1)
             d, m = step2(x, j)
-            send(q, "u", [(j, d, m, "r%d" % ci, "sr%d_%d" % (ci, j))])
+            send(q, "u", [(PIECES[j], d, m, "r%d" % ci, "sr%d_%d" % (ci, j))])
 
     far = sorted([yy for yy in chips if yy != x],
                  key=lambda yy: 0 if (topo.mates(yy, x) or topo.same_plane(yy, x)) else 1)
@@ -300,7 +308,7 @@ def rank_program(g, core, T, topo):
             job = add_up(w0, w1, parts)
             q = pack(take_out(job, w0, w1, T.vt), "v", w0, w1)
             d, m = step3(x, j)
-            send(q, "v", [(j, d, m, "f", "sf%d" % j)])
+            send(q, "v", [(PIECES[j], d, m, "f", "sf%d" % j)])
             if is_rank:
                 store(take_out(job, w0, w1, T.yt), w0, w1)
 

@@ -4,6 +4,9 @@ from concourse.mybir import dt, AluOpType, ActivationFunctionType
 W = 384
 PIECES = [(0, 128), (128, 256), (256, 384)]
 NP = 3
+KEPT = [1, 2]
+DIRECT = 0
+ORDER = KEPT + [DIRECT]
 NX = 90
 
 
@@ -64,36 +67,50 @@ def _plan(T, topo):
     def free(c):
         return all(topo.may_write(c, d) for d in cores if d != c)
 
-    owner, agent, pal = {}, {}, {}
+    agents, owners, pal, pals = {}, {}, {}, {}
     for x in chips:
-        used = []
+        used, busy = [], {}
+        for r in ranks[x]:
+            if free(r):
+                busy[topo.die(r)] = busy.get(topo.die(r), 0) + 1
 
-        def helper(die):
-            h = [c for c in range(topo.CHIPS * topo.CORES_PER_CHIP) if topo.chip(c) == x and topo.die(c) == die
-                 and c not in cores and c not in used and free(c)][0]
+        def helper():
+            cand = [c for c in range(topo.CHIPS * topo.CORES_PER_CHIP) if topo.chip(c) == x
+                    and c not in cores and c not in used and free(c)]
+            h = min(cand, key=lambda c: busy.get(topo.die(c), 0))
             used.append(h)
+            busy[topo.die(h)] = busy.get(topo.die(h), 0) + 1
             return h
 
-        owner[x] = list(ranks[x])
-        agent[x] = [r if free(r) else helper(topo.die(r)) for r in ranks[x]]
-        early = [r for r in ranks[x] if free(r)] + list(ranks[x])
-        h = helper(topo.die(early[0]))
-        owner[x].append(h)
-        agent[x].append(h)
+        agents[x], owners[x] = {}, {}
+        for j in KEPT:
+            h = helper()
+            agents[x][j], owners[x][j] = [h], [h]
+        agents[x][DIRECT] = [r if free(r) else helper() for r in ranks[x]]
+        owners[x][DIRECT] = list(ranks[x])
         for r in ranks[x]:
-            left = [c for c in used if c not in pal]
-            p = ([c for c in left if topo.die(c) == topo.die(r)] + left)[0]
-            pal[r], pal[p] = p, r
-    return chips, ranks, owner, agent, pal
+            pals[r] = []
+        for h in used:
+            same = [r for r in ranks[x] if topo.die(r) == topo.die(h)]
+            r = min(same or ranks[x], key=lambda r: len(pals[r]))
+            pals[r].append(h)
+        for r in ranks[x]:
+            if not pals[r]:
+                rich = max(ranks[x], key=lambda q: len(pals[q]))
+                pals[r].append(pals[rich].pop())
+        for r in ranks[x]:
+            for h in pals[r]:
+                pal[h] = r
+    return chips, ranks, agents, owners, pal, pals
 
 
 def rank_program(g, core, T, topo):
-    chips, ranks, owner, agent, pal = _plan(T, topo)
+    chips, ranks, agents, owners, pal, pals = _plan(T, topo)
     x = topo.chip(core)
     if x not in chips:
         return
     is_rank = T.rank_of(core) is not None
-    if not is_rank and core not in agent[x] and core not in owner[x]:
+    if not is_rank and core not in pal:
         return
     Q = {"t": g.tensor, "v": g.vector, "s": g.scalar, "y": g.sync, "g": g}
     st = {"n": 0, "set": 0, "free": [[], []], "loc": 0, "seen": {}}
@@ -107,62 +124,40 @@ def rank_program(g, core, T, topo):
             st["seen"][(q, name)] = val
             Q[q].wait_ge(T.sem[name], val)
 
-    def outside(xx, j):
-        return agent[xx][j] not in ranks[xx]
+    def full(src, dests):
+        m = _common(topo, src, dests)
+        return _pick(m, _pow2(_bits(m)))
 
-    def step1(xx, k):
+    def step1(xx, k, j):
         r = ranks[xx][k]
-        groups = {"early": [], "again": [], "late": []}
-        for j in range(NP):
-            a, o = agent[xx][j], owner[xx][j]
-            if outside(xx, j):
-                groups["early"].append((j, [a]))
-                if o != a and o != r:
-                    groups["again"].append((j, [o]))
-            else:
-                d = []
-                for c in (a, o):
-                    if c != r and c not in d:
-                        d.append(c)
-                if d:
-                    groups["late"].append((j, d))
-        out = []
-        for kind in ("early", "again", "late"):
-            grp = groups[kind]
-            if grp:
-                m = _common(topo, r, [c for (_, d) in grp for c in d])
-                per = _pow2(_bits(m) // len(grp))
-                out.append((kind, [(j, d, _pick(m, per, per * i)) for i, (j, d) in enumerate(grp)]))
-        return out
+        d = []
+        for c in agents[xx][j] + owners[xx][j]:
+            if c != r and c not in d:
+                d.append(c)
+        return d, full(r, d)
 
-    def count1(xx, k, j):
-        return [2 * _bits(m) for (_, grp) in step1(xx, k) for (jj, d, m) in grp if jj == j and core in d][0]
-
-    def step2(xx, j):
-        d = [owner[yy][j] for yy in chips if yy != xx]
-        m = _common(topo, agent[xx][j], d)
-        return d, _pick(m, _pow2(_bits(m)))
+    def step2(xx, j, i):
+        n = chips.index(xx)
+        d = [owners[yy][j][i] for yy in chips[n + 1:] + chips[:n]]
+        return d, full(agents[xx][j][i], d)
 
     def step3(xx, j):
-        d = [c for c in ranks[xx] if c != owner[xx][j]]
-        m = _common(topo, owner[xx][j], d)
-        return d, _pick(m, _pow2(_bits(m)))
+        d = list(ranks[xx])
+        return d, full(owners[xx][j][0], d)
 
     if is_rank:
-        first = [j for j in range(NP) if outside(x, j)]
-        b_parts = [(min(PIECES[j][0] for j in first), max(PIECES[j][1] for j in first))]
-        b_parts += [PIECES[j] for j in range(NP) if j not in first]
+        b_parts = [PIECES[j] for j in ORDER]
         loads = [(T.bt, T.b, 4 * b_parts[0][0], 4 * b_parts[0][1])]
         loads += [(T.at, T.a, 512 * i, 512 * i + 512) for i in range(4)]
         loads += [(T.bt, T.b, 4 * w0, 4 * w1) for (w0, w1) in b_parts[1:]]
         ld = []
         for i, (dst, src, c0, c1) in enumerate(loads):
             ld.append(new())
-            (g.sync if i % 2 == 0 or i > 4 else g.scalar).dma_start(dst[:, c0:c1], src[:, c0:c1]).then_inc(T.sem[ld[i]], 16)
+            (g.sync if i % 2 == 0 else g.scalar).dma_start(dst[:, c0:c1], src[:, c0:c1]).then_inc(T.sem[ld[i]], 16)
 
-    def send(q, name, trs):
+    def send(q, name, trs, kinds=("c", "p")):
         wait("g", q, 1)
-        for kind in ("c", "p"):
+        for kind in kinds:
             lst = []
             for ((w0, w1), dests, mask, land, sem) in trs:
                 src, dst = T[name + kind][:, w0:w1], T[land + kind][:, w0:w1]
@@ -189,12 +184,15 @@ def rank_program(g, core, T, topo):
         wait("v", s_sh, 3)
     g.vector.quantize_mx(T.selc[:, made[0]:made[1]], T.selp[:, made[0]:made[1]],
                          T.selt[:, 4 * made[0]:4 * made[1]]).then_inc(T.sem[s_sel], 1)
-
-    def swap_mask(src):
-        m = topo.mask(src, pal[src])
-        return _pick(m, _pow2(_bits(m)))
-
-    send(s_sel, "sel", [(made, [pal[core]], swap_mask(core), "sel", "sp")])
+    if is_rank:
+        send(s_sel, "sel", [(made, pals[core], full(core, pals[core]), "sel", "sp")])
+        sp_all = sum(2 * _bits(full(h, [core])) for h in pals[core])
+    else:
+        team = pals[pal[core]]
+        n, i = len(team), team.index(core)
+        share = (128 * (1 + (3 * i) // n), 128 * (1 + (3 * (i + 1)) // n))
+        send(s_sel, "sel", [(share, [pal[core]], full(core, [pal[core]]), "sel", "sp")])
+        sp_all = 2 * _bits(full(pal[core], team))
 
     q_b, q_a = [], []
 
@@ -229,7 +227,7 @@ def rank_program(g, core, T, topo):
                     lc, lp, rc, rp = T.ac, T.ap, T.bc, T.bp
                 else:
                     wait("t", s_sel, 1)
-                    wait("t", "sp", 2 * _bits(swap_mask(pal[core])))
+                    wait("t", "sp", sp_all)
                     wait("t", part[1], part[2])
                     lc, lp, rc, rp = T.selc, T.selp, T[part[0] + "c"], T[part[0] + "p"]
                 c0 = 512 * (4 * s + t)
@@ -263,7 +261,9 @@ def rank_program(g, core, T, topo):
         return q
 
     def chip_parts(j):
-        return [None if r == core else ("l%d" % k, "sl%d_%d" % (k, j), count1(x, k, j)) for k, r in enumerate(ranks[x])]
+        parts = [None] if is_rank else []
+        return parts + [("l%d" % k, "sl%d_%d" % (k, j), 2 * _bits(step1(x, k, j)[1]))
+                        for k, r in enumerate(ranks[x]) if r != core]
 
     stores = []
 
@@ -275,45 +275,42 @@ def rank_program(g, core, T, topo):
 
     if is_rank:
         k = ranks[x].index(core)
-        packed = {}
-        for kind, grp in step1(x, k):
-            if kind == "late":
-                for n in range(1, len(b_parts)):
-                    pack_b(n, ld[4 + n])
-            if kind != "again":
-                w0, w1 = min(PIECES[j][0] for (j, _, _) in grp), max(PIECES[j][1] for (j, _, _) in grp)
-                q = pack(take_out(add_up(w0, w1, [None]), w0, w1, T.tt), "t", w0, w1)
-                for (j, _, _) in grp:
-                    packed[j] = q
-            send(packed[grp[0][0]], "t", [(PIECES[j], d, m, "l%d" % k, "sl%d_%d" % (k, j)) for (j, d, m) in grp])
-        for n in range(len(q_b), len(b_parts)):
-            pack_b(n, ld[4 + n])
+        for n, j in enumerate(ORDER):
+            if n > 0:
+                pack_b(n, ld[4 + n])
+            w0, w1 = PIECES[j]
+            q = pack(take_out(add_up(w0, w1, [None]), w0, w1, T.tt), "t", w0, w1)
+            d, m = step1(x, k, j)
+            send(q, "t", [(PIECES[j], d, m, "l%d" % k, "sl%d_%d" % (k, j))])
 
     ci = chips.index(x)
-    for j in range(NP):
-        if agent[x][j] == core:
-            w0, w1 = PIECES[j]
-            q = pack(take_out(add_up(w0, w1, chip_parts(j)), w0, w1, T.ut), "u", w0, w1)
-            d, m = step2(x, j)
-            send(q, "u", [(PIECES[j], d, m, "r%d" % ci, "sr%d_%d" % (ci, j))])
+    for j in ORDER:
+        for i, a in enumerate(agents[x][j]):
+            if a == core:
+                w0, w1 = PIECES[j]
+                q = pack(take_out(add_up(w0, w1, chip_parts(j)), w0, w1, T.ut), "u", w0, w1)
+                d, m = step2(x, j, i)
+                send(q, "u", [(PIECES[j], d, m, "r%d" % ci, "sr%d_%d" % (ci, j))], ("p", "c"))
 
-    far = sorted([yy for yy in chips if yy != x],
-                 key=lambda yy: 0 if (topo.mates(yy, x) or topo.same_plane(yy, x)) else 1)
-    for j in range(NP):
-        if owner[x][j] == core:
-            w0, w1 = PIECES[j]
-            parts = chip_parts(j)
-            for yy in far:
-                parts.append(("r%d" % chips.index(yy), "sr%d_%d" % (chips.index(yy), j), 2 * _bits(step2(yy, j)[1])))
-            job = add_up(w0, w1, parts)
-            q = pack(take_out(job, w0, w1, T.vt), "v", w0, w1)
-            d, m = step3(x, j)
-            send(q, "v", [(PIECES[j], d, m, "f", "sf%d" % j)])
-            if is_rank:
-                store(take_out(job, w0, w1, T.yt), w0, w1)
+    far = [chips[ci - n] for n in range(1, len(chips))]
+    for j in ORDER:
+        for i, o in enumerate(owners[x][j]):
+            if o == core:
+                w0, w1 = PIECES[j]
+                parts = chip_parts(j)
+                for yy in far:
+                    parts.append(("r%d" % chips.index(yy), "sr%d_%d" % (chips.index(yy), j),
+                                  2 * _bits(step2(yy, j, i)[1])))
+                job = add_up(w0, w1, parts)
+                if is_rank:
+                    store(take_out(job, w0, w1, T.yt), w0, w1)
+                else:
+                    q = pack(take_out(job, w0, w1, T.vt), "v", w0, w1)
+                    d, m = step3(x, j)
+                    send(q, "v", [(PIECES[j], d, m, "f", "sf%d" % j)])
 
     if is_rank:
-        for j in sorted([j for j in range(NP) if owner[x][j] != core], key=lambda j: 1 if outside(x, j) else 0):
+        for j in KEPT:
             w0, w1 = PIECES[j]
             job = add_up(w0, w1, [("f", "sf%d" % j, 2 * _bits(step3(x, j)[1]))])
             store(take_out(job, w0, w1, T.yt), w0, w1)

@@ -83,9 +83,9 @@ def _plan(T, topo):
             return h
 
         agents[x], owners[x] = {}, {}
-        for j in KEPT:
-            h = helper()
-            agents[x][j], owners[x][j] = [h], [h]
+        keep = [helper() for _ in KEPT]
+        for n, j in enumerate(KEPT):
+            agents[x][j], owners[x][j] = [keep[n], keep[(n + 1) % len(keep)]], [keep[n]]
         agents[x][DIRECT] = [r if free(r) else helper() for r in ranks[x]]
         owners[x][DIRECT] = list(ranks[x])
         for r in ranks[x]:
@@ -134,11 +134,19 @@ def rank_program(g, core, T, topo):
         for c in agents[xx][j] + owners[xx][j]:
             if c != r and c not in d:
                 d.append(c)
+        if j == DIRECT:
+            d.sort(key=lambda c: T.rank_of(c) is not None)
         return d, full(r, d)
 
-    def step2(xx, j, i):
+    def turn(xx):
         n = chips.index(xx)
-        d = [owners[yy][j][i] for yy in chips[n + 1:] + chips[:n]]
+        return chips[n + 1:] + chips[:n]
+
+    def step2(xx, j, i):
+        if j in KEPT:
+            d = [owners[yy][j][0] for yy in (turn(xx)[:-1] if i == 0 else turn(xx)[-1:])]
+        else:
+            d = [owners[yy][j][i] for yy in turn(xx)]
         return d, full(agents[xx][j][i], d)
 
     def step3(xx, j):
@@ -148,7 +156,7 @@ def rank_program(g, core, T, topo):
     if is_rank:
         b_parts = [PIECES[j] for j in ORDER]
         loads = [(T.bt, T.b, 4 * b_parts[0][0], 4 * b_parts[0][1])]
-        loads += [(T.at, T.a, 512 * i, 512 * i + 512) for i in range(4)]
+        loads += [(T.at, T.a, 1024 * i, 1024 * i + 1024) for i in range(2)]
         loads += [(T.bt, T.b, 4 * w0, 4 * w1) for (w0, w1) in b_parts[1:]]
         ld = []
         for i, (dst, src, c0, c1) in enumerate(loads):
@@ -204,11 +212,11 @@ def rank_program(g, core, T, topo):
 
     if is_rank:
         pack_b(0, ld[0])
-        for i in range(4):
+        for i in range(2):
             q_a.append(new())
             wait("v", ld[1 + i], 16)
-            g.vector.quantize_mx(T.ac[:, 128 * i:128 * i + 128], T.ap[:, 128 * i:128 * i + 128],
-                                 T.at[:, 512 * i:512 * i + 512]).then_inc(T.sem[q_a[i]], 1)
+            g.vector.quantize_mx(T.ac[:, 256 * i:256 * i + 256], T.ap[:, 256 * i:256 * i + 256],
+                                 T.at[:, 1024 * i:1024 * i + 1024]).then_inc(T.sem[q_a[i]], 1)
 
     def add_up(w0, w1, parts):
         s = st["set"]
@@ -223,7 +231,7 @@ def rank_program(g, core, T, topo):
                     for (v0, v1, sem) in q_b:
                         if v0 < w1 and w0 < v1:
                             wait("t", sem, 1)
-                    wait("t", q_a[t], 1)
+                    wait("t", q_a[t // 2], 1)
                     lc, lp, rc, rp = T.ac, T.ap, T.bc, T.bp
                 else:
                     wait("t", s_sel, 1)
@@ -276,10 +284,11 @@ def rank_program(g, core, T, topo):
     if is_rank:
         k = ranks[x].index(core)
         for n, j in enumerate(ORDER):
-            if n > 0:
-                pack_b(n, ld[4 + n])
             w0, w1 = PIECES[j]
-            q = pack(take_out(add_up(w0, w1, [None]), w0, w1, T.tt), "t", w0, w1)
+            cp = take_out(add_up(w0, w1, [None]), w0, w1, T.tt)
+            if n + 1 < len(ORDER):
+                pack_b(n + 1, ld[3 + n])
+            q = pack(cp, "t", w0, w1)
             d, m = step1(x, k, j)
             send(q, "t", [(PIECES[j], d, m, "l%d" % k, "sl%d_%d" % (k, j))])
 
@@ -292,15 +301,19 @@ def rank_program(g, core, T, topo):
                 d, m = step2(x, j, i)
                 send(q, "u", [(PIECES[j], d, m, "r%d" % ci, "sr%d_%d" % (ci, j))], ("p", "c"))
 
-    far = [chips[ci - n] for n in range(1, len(chips))]
     for j in ORDER:
         for i, o in enumerate(owners[x][j]):
             if o == core:
                 w0, w1 = PIECES[j]
                 parts = chip_parts(j)
-                for yy in far:
-                    parts.append(("r%d" % chips.index(yy), "sr%d_%d" % (chips.index(yy), j),
-                                  2 * _bits(step2(yy, j, i)[1])))
+                due = []
+                for yy in turn(x):
+                    for n in (range(len(agents[yy][j])) if j in KEPT else [i]):
+                        d, m = step2(yy, j, n)
+                        if core in d:
+                            due.append((d.index(core), turn(yy).index(x), yy, m))
+                for (_, _, yy, m) in sorted(due):
+                    parts.append(("r%d" % chips.index(yy), "sr%d_%d" % (chips.index(yy), j), 2 * _bits(m)))
                 job = add_up(w0, w1, parts)
                 if is_rank:
                     store(take_out(job, w0, w1, T.yt), w0, w1)

from concourse.bass import DstId, RemoteDMATransfer
from concourse.mybir import dt, AluOpType, ActivationFunctionType

W = 384
PIECES = [(0, 128), (128, 256), (256, 384)]
NP = 3
KEPT = [1, 2]
DIRECT = 0
ORDER = KEPT + [DIRECT]
NX = 90


def _pair(name, n):
    return {name + "c": ("sbuf", [128, n], "float8_e4m3fn_x4"), name + "p": ("sbuf", [128, n], "uint8")}


SCRATCH = {
    "at": ("sbuf", [128, 2048], "bfloat16"),
    "bt": ("sbuf", [128, 1536], "bfloat16"),
    "ones": ("sbuf", [128, 512], "bfloat16"),
    "selt": ("sbuf", [128, 2048], "bfloat16"),
    "tt": ("sbuf", [128, 1536], "bfloat16"),
    "ut": ("sbuf", [128, 1536], "bfloat16"),
    "vt": ("sbuf", [128, 1536], "bfloat16"),
    "yt": ("sbuf", [128, 1536], "float32"),
    "ps": ("psum", [128, 4096], "float32"),
}
for _n, _w in (("a", 512), ("b", W), ("sel", 512), ("t", W), ("u", W), ("v", W), ("l0", W), ("l1", W),
               ("r0", W), ("r1", W), ("r2", W), ("r3", W), ("f", W)):
    SCRATCH.update(_pair(_n, _w))

SEMAPHORES = (["x%d" % i for i in range(NX)] + ["sl%d_%d" % (k, j) for k in range(2) for j in range(NP)]
              + ["sr%d_%d" % (c, j) for c in range(4) for j in range(NP)] + ["sf%d" % j for j in range(NP)] + ["sp", "loc"])


def _bits(mask):
    return bin(mask).count("1")


def _pick(mask, k, skip=0):
    on = [i for i in range(mask.bit_length()) if (mask >> i) & 1]
    return sum(1 << i for i in on[skip:skip + k])


def _common(topo, src, dests):
    m = topo.mask(src, dests[0])
    for d in dests[1:]:
        m &= topo.mask(src, d)
    return m


def _pow2(n):
    p = 1
    while 2 * p <= n:
        p *= 2
    return p


def _plan(T, topo):
    cores = list(T.cores)
    chips = []
    for c in cores:
        if topo.chip(c) not in chips:
            chips.append(topo.chip(c))
    ranks = {x: [c for c in cores if topo.chip(c) == x] for x in chips}

    def free(c):
        return all(topo.may_write(c, d) for d in cores if d != c)

    agents, owners, pal, pals = {}, {}, {}, {}
    for x in chips:
        used, busy = [], {}
        for r in ranks[x]:
            if free(r):
                busy[topo.die(r)] = busy.get(topo.die(r), 0) + 1

        def helper():
            cand = [c for c in range(topo.CHIPS * topo.CORES_PER_CHIP) if topo.chip(c) == x
                    and c not in cores and c not in used and free(c)]
            h = min(cand, key=lambda c: busy.get(topo.die(c), 0))
            used.append(h)
            busy[topo.die(h)] = busy.get(topo.die(h), 0) + 1
            return h

        agents[x], owners[x] = {}, {}
        keep = [helper() for _ in KEPT]
        for n, j in enumerate(KEPT):
            agents[x][j], owners[x][j] = [keep[n], keep[(n + 1) % len(keep)]], [keep[n]]
        agents[x][DIRECT] = [r if free(r) else helper() for r in ranks[x]]
        owners[x][DIRECT] = list(ranks[x])
        for r in ranks[x]:
            pals[r] = []
        for h in used:
            same = [r for r in ranks[x] if topo.die(r) == topo.die(h)]
            r = min(same or ranks[x], key=lambda r: len(pals[r]))
            pals[r].append(h)
        for r in ranks[x]:
            if not pals[r]:
                rich = max(ranks[x], key=lambda q: len(pals[q]))
                pals[r].append(pals[rich].pop())
        for r in ranks[x]:
            for h in pals[r]:
                pal[h] = r
    return chips, ranks, agents, owners, pal, pals


def rank_program(g, core, T, topo):
    chips, ranks, agents, owners, pal, pals = _plan(T, topo)
    x = topo.chip(core)
    if x not in chips:
        return
    is_rank = T.rank_of(core) is not None
    if not is_rank and core not in pal:
        return
    Q = {"t": g.tensor, "v": g.vector, "s": g.scalar, "y": g.sync, "g": g}
    st = {"n": 0, "set": 0, "free": [[], []], "loc": 0, "seen": {}}

    def new():
        st["n"] += 1
        return "x%d" % (st["n"] - 1)

    def wait(q, name, val):
        if st["seen"].get((q, name), 0) < val:
            st["seen"][(q, name)] = val
            Q[q].wait_ge(T.sem[name], val)

    def full(src, dests):
        m = _common(topo, src, dests)
        return _pick(m, _pow2(_bits(m)))

    def step1(xx, k, j):
        r = ranks[xx][k]
        d = []
        for c in agents[xx][j] + owners[xx][j]:
            if c != r and c not in d:
                d.append(c)
        if j == DIRECT:
            d.sort(key=lambda c: T.rank_of(c) is not None)
        return d, full(r, d)

    def turn(xx):
        n = chips.index(xx)
        return chips[n + 1:] + chips[:n]

    def step2(xx, j, i):
        if j in KEPT:
            d = [owners[yy][j][0] for yy in (turn(xx)[:-1] if i == 0 else turn(xx)[-1:])]
        else:
            d = [owners[yy][j][i] for yy in turn(xx)]
        return d, full(agents[xx][j][i], d)

    def step3(xx, j):
        d = list(ranks[xx])
        return d, full(owners[xx][j][0], d)

    if is_rank:
        b_parts = [PIECES[j] for j in ORDER]
        loads = [(T.bt, T.b, 4 * b_parts[0][0], 4 * b_parts[0][1])]
        loads += [(T.at, T.a, 1024 * i, 1024 * i + 1024) for i in range(2)]
        loads += [(T.bt, T.b, 4 * w0, 4 * w1) for (w0, w1) in b_parts[1:]]
        ld = []
        for i, (dst, src, c0, c1) in enumerate(loads):
            ld.append(new())
            (g.sync if i % 2 == 0 else g.scalar).dma_start(dst[:, c0:c1], src[:, c0:c1]).then_inc(T.sem[ld[i]], 16)

    def send(q, name, trs, kinds=("c", "p")):
        wait("g", q, 1)
        for kind in kinds:
            lst = []
            for ((w0, w1), dests, mask, land, sem) in trs:
                src, dst = T[name + kind][:, w0:w1], T[land + kind][:, w0:w1]
                if kind == "c":
                    src, dst = src.bitcast(dt.uint8), dst.bitcast(dt.uint8)
                lst.append(RemoteDMATransfer(dst_ids=[DstId(rid=topo.addr(d)[0], pnc=topo.addr(d)[1]) for d in dests],
                                             dma_engine_mask=mask, remote_sem=T.sem[sem], srcs=[src],
                                             dsts=[dst for _ in dests]))
                st["loc"] += _bits(mask)
            g.remote_dma_fused(lst, local_sem=T.sem.loc)

    s_one, s_zero, s_aff, s_sh, s_sel = new(), new(), new(), new(), new()
    g.vector.memset(T.ones[:, :], 1.0).then_inc(T.sem[s_one], 1)
    if not is_rank:
        g.vector.memset(T.selt[:, 512:2048], 0.0).then_inc(T.sem[s_zero], 1)
    wait("g", s_one, 1)
    g.affine_select(T.selt[:, 0:512], T.ones[:, :], [[-1, 512]], AluOpType.is_equal, 0.0, 0, 4).then_inc(T.sem[s_aff], 1)
    wait("v", s_aff, 1)
    made = (0, 128) if is_rank else (128, 512)
    if not is_rank:
        wait("v", s_zero, 1)
        for t in range(1, 4):
            g.vector.tensor_copy(T.selt[:, 512 * t + t:512 * t + 512], T.selt[:, 0:512 - t]).then_inc(T.sem[s_sh], 1)
        wait("v", s_sh, 3)
    g.vector.quantize_mx(T.selc[:, made[0]:made[1]], T.selp[:, made[0]:made[1]],
                         T.selt[:, 4 * made[0]:4 * made[1]]).then_inc(T.sem[s_sel], 1)
    if is_rank:
        send(s_sel, "sel", [(made, pals[core], full(core, pals[core]), "sel", "sp")])
        sp_all = sum(2 * _bits(full(h, [core])) for h in pals[core])
    else:
        team = pals[pal[core]]
        n, i = len(team), team.index(core)
        share = (128 * (1 + (3 * i) // n), 128 * (1 + (3 * (i + 1)) // n))
        send(s_sel, "sel", [(share, [pal[core]], full(core, [pal[core]]), "sel", "sp")])
        sp_all = 2 * _bits(full(pal[core], team))

    q_b, q_a = [], []

    def pack_b(i, sem):
        w0, w1 = b_parts[i]
        q_b.append((w0, w1, new()))
        wait("v", sem, 16)
        g.vector.quantize_mx(T.bc[:, w0:w1], T.bp[:, w0:w1], T.bt[:, 4 * w0:4 * w1]).then_inc(T.sem[q_b[-1][2]], 1)

    if is_rank:
        pack_b(0, ld[0])
        for i in range(2):
            q_a.append(new())
            wait("v", ld[1 + i], 16)
            g.vector.quantize_mx(T.ac[:, 256 * i:256 * i + 256], T.ap[:, 256 * i:256 * i + 256],
                                 T.at[:, 1024 * i:1024 * i + 1024]).then_inc(T.sem[q_a[i]], 1)

    def add_up(w0, w1, parts):
        s = st["set"]
        st["set"] = 1 - s
        for (name, val) in st["free"][s]:
            wait("t", name, val)
        st["free"][s] = []
        done = [new() for _ in range(4)]
        for k, part in enumerate(parts):
            for t in range(4):
                if part is None:
                    for (v0, v1, sem) in q_b:
                        if v0 < w1 and w0 < v1:
                            wait("t", sem, 1)
                    wait("t", q_a[t // 2], 1)
                    lc, lp, rc, rp = T.ac, T.ap, T.bc, T.bp
                else:
                    wait("t", s_sel, 1)
                    wait("t", "sp", sp_all)
                    wait("t", part[1], part[2])
                    lc, lp, rc, rp = T.selc, T.selp, T[part[0] + "c"], T[part[0] + "p"]
                c0 = 512 * (4 * s + t)
                ins = g.tensor.matmul_mx(T.ps[:, c0:c0 + w1 - w0], lc[:, 128 * t:128 * t + 128],
                                         lp[:, 128 * t:128 * t + 128], rc[:, w0:w1], rp[:, w0:w1],
                                         k == 0, k == len(parts) - 1)
                if k == len(parts) - 1:
                    ins.then_inc(T.sem[done[t]], 1)
        return s, done

    def take_out(job, w0, w1, tile):
        s, done = job
        cp = new()
        for t in range(4):
            c0 = 512 * (4 * s + t)
            src, dst = T.ps[:, c0:c0 + w1 - w0], tile[:, 4 * w0 + t:4 * w1:4]
            if t % 2 == 0:
                wait("s", done[t], 1)
                g.scalar.activation(dst, src, ActivationFunctionType.Copy).then_inc(T.sem[cp], 1)
            else:
                wait("v", done[t], 1)
                g.vector.tensor_copy(dst, src).then_inc(T.sem[cp], 1)
        st["free"][s].append((cp, 4))
        return cp

    def pack(cp, name, w0, w1):
        q = new()
        wait("v", cp, 4)
        g.vector.quantize_mx(T[name + "c"][:, w0:w1], T[name + "p"][:, w0:w1],
                             T[name + "t"][:, 4 * w0:4 * w1]).then_inc(T.sem[q], 1)
        return q

    def chip_parts(j):
        parts = [None] if is_rank else []
        return parts + [("l%d" % k, "sl%d_%d" % (k, j), 2 * _bits(step1(x, k, j)[1]))
                        for k, r in enumerate(ranks[x]) if r != core]

    stores = []

    def store(cp, w0, w1):
        s = new()
        wait("y", cp, 4)
        g.sync.dma_start(T.y[:, 4 * w0:4 * w1], T.yt[:, 4 * w0:4 * w1]).then_inc(T.sem[s], 16)
        stores.append(s)

    if is_rank:
        k = ranks[x].index(core)
        for n, j in enumerate(ORDER):
            w0, w1 = PIECES[j]
            cp = take_out(add_up(w0, w1, [None]), w0, w1, T.tt)
            if n + 1 < len(ORDER):
                pack_b(n + 1, ld[3 + n])
            q = pack(cp, "t", w0, w1)
            d, m = step1(x, k, j)
            send(q, "t", [(PIECES[j], d, m, "l%d" % k, "sl%d_%d" % (k, j))])

    ci = chips.index(x)
    for j in ORDER:
        for i, a in enumerate(agents[x][j]):
            if a == core:
                w0, w1 = PIECES[j]
                q = pack(take_out(add_up(w0, w1, chip_parts(j)), w0, w1, T.ut), "u", w0, w1)
                d, m = step2(x, j, i)
                send(q, "u", [(PIECES[j], d, m, "r%d" % ci, "sr%d_%d" % (ci, j))], ("p", "c"))

    for j in ORDER:
        for i, o in enumerate(owners[x][j]):
            if o == core:
                w0, w1 = PIECES[j]
                parts = chip_parts(j)
                due = []
                for yy in turn(x):
                    for n in (range(len(agents[yy][j])) if j in KEPT else [i]):
                        d, m = step2(yy, j, n)
                        if core in d:
                            due.append((d.index(core), turn(yy).index(x), yy, m))
                for (_, _, yy, m) in sorted(due):
                    parts.append(("r%d" % chips.index(yy), "sr%d_%d" % (chips.index(yy), j), 2 * _bits(m)))
                job = add_up(w0, w1, parts)
                if is_rank:
                    store(take_out(job, w0, w1, T.yt), w0, w1)
                else:
                    q = pack(take_out(job, w0, w1, T.vt), "v", w0, w1)
                    d, m = step3(x, j)
                    send(q, "v", [(PIECES[j], d, m, "f", "sf%d" % j)])

    if is_rank:
        for j in KEPT:
            w0, w1 = PIECES[j]
            job = add_up(w0, w1, [("f", "sf%d" % j, 2 * _bits(step3(x, j)[1]))])
            store(take_out(job, w0, w1, T.yt), w0, w1)

    wait("g", "loc", st["loc"])
    for s in stores:
        wait("y", s, 16)
